import numpy as np
import ml_dtypes


def mxq(x, axis, fmt="e4m3"):
    dtype, down = {"e4m3": (ml_dtypes.float8_e4m3fn, 7), "e5m2": (ml_dtypes.float8_e5m2, 14)}[fmt]
    v = np.moveaxis(np.asarray(x, np.float32).astype(ml_dtypes.bfloat16).astype(np.float64), axis, -1)
    blocks = v.reshape(v.shape[:-1] + (-1, 32))
    amax = np.abs(blocks).max(-1, keepdims=True)
    byte = np.maximum(np.where(amax > 0, np.frexp(amax)[1] - 1 + 127, 0) - down, 1)
    scale = np.exp2(byte - 127.0)
    codes = (blocks / scale).astype(np.float32).astype(dtype).astype(np.float64)
    return np.moveaxis((codes * scale).reshape(v.shape), -1, axis)


WIDE = False


def mx_kscale(k):
    if not WIDE:
        return np.ones(k)
    levels = np.array([30, -30])
    if k % 512:
        return np.exp2(np.random.permutation(np.resize(levels, k // 32))).repeat(32)
    a = np.empty((k // 512, 16))
    for p in range(k // 512):
        a[p, :8] = np.random.permutation(np.resize(levels, 8))
        for g in range(8):
            far = levels[np.abs(levels - a[p, g]) >= 10]
            a[p, g + 8] = far[np.random.randint(len(far))]
    return np.exp2(a.ravel()).repeat(32)


def f64(x):
    return np.asarray(x).astype(np.float64)


def striped(idx):
    return np.tile(np.asarray(idx).reshape(-1, 16).T, (8, 1)).astype(np.uint16)


def unstriped(offs):
    return offs[:16].T.reshape(-1).astype(np.int64)


E2M1 = np.array([0.0, 0.5, 1.0, 1.5, 2.0, 3.0, 4.0, 6.0, -0.0, -0.5, -1.0, -1.5, -2.0, -3.0, -4.0, -6.0])


def pack_weight(w, fmt):
    k, n = w.shape
    w = f64(np.asarray(w, np.float32).astype(ml_dtypes.bfloat16)).reshape(k // 32, 32, n)
    amax = np.abs(w).max(1)
    if fmt in ("e4m3", "e5m2"):
        byte = np.frexp(amax)[1] - 1 + 127 - (7 if fmt == "e4m3" else 14)
    else:
        mant, ex = np.frexp(amax / 6.0)
        byte = np.where(mant > 0.5, ex, ex - 1) + 127
    byte = np.clip(np.where(amax > 0, byte, 1), 1, 254)
    scaled = (w * np.exp2(127.0 - byte)[:, None, :]).reshape(k, n).astype(np.float32)
    by_word = np.ascontiguousarray(scaled.reshape(k // 512, 128, 4, n).transpose(0, 1, 3, 2))
    if fmt in ("e4m3", "e5m2"):
        words = by_word.astype(ml_dtypes.float8_e4m3fn if fmt == "e4m3" else ml_dtypes.float8_e5m2).view(np.uint8)
    else:
        c = by_word.astype(ml_dtypes.float4_e2m1fn).view(np.uint8) & 0xF
        words = (c[..., 0::2] | (c[..., 1::2] << 4)).reshape(k // 512, 128, 2 * n)
    return np.ascontiguousarray(words), np.ascontiguousarray(byte.astype(np.uint8).reshape(k // 512, 16, n))


def unpack_weight(words, scales, fmt):
    g, _, n = scales.shape
    words = np.ascontiguousarray(words).reshape(g, 128, n, -1)
    if fmt in ("e4m3", "e5m2"):
        vals = words.view(ml_dtypes.float8_e4m3fn if fmt == "e4m3" else ml_dtypes.float8_e5m2).astype(np.float64)
    else:
        nib = np.empty((g, 128, n, 4), np.uint8)
        nib[..., 0::2] = words & 0xF
        nib[..., 1::2] = words >> 4
        vals = E2M1[nib]
    vals = vals * np.repeat(np.exp2(scales.astype(np.float64) - 127.0), 8, axis=1)[..., None]
    return vals.transpose(0, 1, 3, 2).reshape(g * 512, n)


def sigmoid(v):
    return 1.0 / (1.0 + np.exp(-v))


K, T, J, R, F, Z, O, N, S, E = 512, 1024, 256, 512, 512, 1024, 128, 256, 1024, 1024


def setup_inputs():
    n = np.random.standard_normal
    idx = np.random.permutation(T)[:J]
    idx2 = np.random.permutation(Z)[:J]
    idx3 = np.random.permutation(J)[:O]
    idx4 = np.random.permutation(J)[:O]
    idx5 = np.random.permutation(J)[:O]
    idx6 = np.random.permutation(S)[:N]
    idx7 = np.random.permutation(E)[:O]
    fk = mx_kscale(K)
    ff = mx_kscale(F)
    fr = mx_kscale(R)
    xtp = pack_weight(n((K, T)) / fk[:, None], "e2m1")
    xop = pack_weight(n((F, Z)) / ff[:, None], "e5m2")
    wp = pack_weight(n((K, R)) * 1 / np.sqrt(K) * fk[:, None], "e5m2")
    w0p = pack_weight(n((F, R)) * 1 / np.sqrt(F) * ff[:, None], "e4m3")
    w2p = pack_weight(n((F, R)) * 1 / np.sqrt(F) * ff[:, None], "e4m3")
    vsp = pack_weight(n((R, S)) * 1 / np.sqrt(R) / fr[:, None], "e4m3")
    return {
        "xt_words": xtp[0],
        "xt_scales": xtp[1],
        "xo_words": xop[0],
        "xo_scales": xop[1],
        "w_words": wp[0],
        "w_scales": wp[1],
        "w0_words": w0p[0],
        "w0_scales": w0p[1],
        "w2_words": w2p[0],
        "w2_scales": w2p[1],
        "sa": (np.random.uniform(0.5, 1.6, (R, 1)) * fr[:, None]).astype(np.float32),
        "sb": (np.random.uniform(0.5, 1.6, (R, 1)) * fr[:, None]).astype(np.float32),
        "bg": (np.random.uniform(-2.0, 2.0, (R, 1))).astype(np.float32),
        "vs_words": vsp[0],
        "vs_scales": vsp[1],
        "offs": striped(idx),
        "offs2": striped(idx2),
        "offs3": striped(idx3),
        "offs4": striped(idx4),
        "offs5": striped(idx5),
        "offs6": striped(idx6),
        "offs7": striped(idx7),
    }


def reference(xt_words, xt_scales, xo_words, xo_scales, w_words, w_scales, w0_words, w0_scales, w2_words, w2_scales, sa, sb, bg, vs_words, vs_scales, offs, offs2, offs3, offs4, offs5, offs6, offs7):
    idx = unstriped(offs)
    idx2 = unstriped(offs2)
    idx3 = unstriped(offs3)
    idx4 = unstriped(offs4)
    idx5 = unstriped(offs5)
    idx6 = unstriped(offs6)
    idx7 = unstriped(offs7)
    xtu = unpack_weight(xt_words, xt_scales, "e2m1")
    xou = unpack_weight(xo_words, xo_scales, "e5m2")
    wu = unpack_weight(w_words, w_scales, "e5m2")
    w0u = unpack_weight(w0_words, w0_scales, "e4m3")
    w2u = unpack_weight(w2_words, w2_scales, "e4m3")
    vsu = unpack_weight(vs_words, vs_scales, "e4m3")
    xtidxg = xtu[:, idx]
    xoidx2g = xou[:, idx2]
    a = wu.T @ xtidxg + w0u.T @ xoidx2g
    b = w2u.T @ xoidx2g
    lb = b[:, 0:1]
    u1 = a[:, idx3] * f64(sa) * sigmoid(a[:, idx4] * lb + f64(bg))
    hid = np.maximum(u1, b[:, idx5] * f64(sb))
    vsidx6g = vsu[:, idx6]
    hidq = mxq(hid, 0, "e5m2")
    p = vsidx6g.T @ hidq
    y = np.zeros((N, E))
    y[:, idx7] = p
    return y

@@ -1,0 +1,197 @@
+from contextlib import ExitStack
+
+import concourse.mybir as mybir
+
+F32 = mybir.dt.float32
+BF16 = mybir.dt.bfloat16
+I32 = mybir.dt.int32
+U32 = mybir.dt.uint32
+U16 = mybir.dt.uint16
+U8 = mybir.dt.uint8
+E4M3 = mybir.dt.float8_e4m3fn_x4
+E5M2 = mybir.dt.float8_e5m2_x4
+E2M1 = mybir.dt.float4_e2m1fn_x4
+ACT = mybir.ActivationFunctionType
+ALU = mybir.AluOpType
+
+P = 128
+PACK = 4
+QUAD = 32
+TABLE = 1024
+R = 512
+J = 256
+O = 128
+N = 256
+E = 1024
+FLOPS = 2 * (3 * 512 * R * J + R * N * O)
+
+
+def tile_list_slopelead_noted_store_scattered_kernel(
+    tc, xt_words, xt_scales, xo_words, xo_scales, w_words, w_scales, w0_words, w0_scales, w2_words, w2_scales,
+    sa, sb, bg, vs_words, vs_scales, offs, offs2, offs3, offs4, offs5, offs6, offs7, out,
+):
+    nc = tc.nc
+    with ExitStack() as ctx:
+        pool = ctx.enter_context(tc.tile_pool(name="held", bufs=1))
+        psum = ctx.enter_context(tc.psum_pool(name="psum", bufs=1))
+
+        def sbuf(name, shape, dtype, tag=""):
+            return pool.tile(shape, dtype, name=name, tag=tag, align_bytes=64)
+
+        def list_tile(name, src):
+            return sbuf(name, list(src.shape), U16)
+
+        def as_words(words):
+            return words[0].rearrange("p c r -> p (c r)").bitcast(I32)
+
+        def scale_rows(scales, q):
+            return scales[0].bitcast(I32)[PACK * q : PACK * (q + 1), :]
+
+        def scale_rows_paired(scales, h):
+            return scales[0].bitcast(I32).rearrange("(half h i) c -> h i half c", half=2, h=2)[h]
+
+        def quad_rows(q):
+            return slice(QUAD * q, QUAD * q + PACK)
+
+        l1, l2, l3, l4 = list_tile("l1", offs), list_tile("l2", offs2), list_tile("l3", offs3), list_tile("l4", offs4)
+        l5, l6, l7 = list_tile("l5", offs5), list_tile("l6", offs6), list_tile("l7", offs7)
+        xt_w = sbuf("xt_w", [P, TABLE], U16)
+        xo_w = sbuf("xo_w", [P, TABLE], U32)
+        vs_w = sbuf("vs_w", [P, TABLE], U32)
+        xt_s = sbuf("xt_s", [P, TABLE], U8)
+        xo_s = sbuf("xo_s", [P, TABLE], U8)
+        vs_s = sbuf("vs_s", [P, TABLE], U8)
+        xo_stage = sbuf("xo_stage", [P // 2, 2, TABLE // 4], I32)
+        w_raw = {g: sbuf(g + "_raw", [P, R], U32) for g in ("w2", "w0", "w")}
+        w_stage = sbuf("w_stage", [P, 2, 3, R // 4], I32, tag="w_stage")
+        sa_t, sb_t, bg_t = sbuf("sa_t", [P, PACK], F32), sbuf("sb_t", [P, PACK], F32), sbuf("bg_t", [P, PACK], F32)
+        pages = [sbuf("page%d" % h, [P, E], F32) for h in range(2)]
+
+        nc.vector.memset(xo_stage[:], 0)
+        nc.vector.memset(w_stage[: P // 2], 0)
+        nc.vector.memset(xt_s[:].bitcast(I32), 0)
+        nc.vector.memset(vs_s[:].bitcast(I32), 0)
+        for page in pages:
+            nc.vector.memset(page[:], 0.0)
+
+        def by_feature(v):
+            return v.rearrange("(p t) o -> p (t o)", t=PACK)
+
+        nc.sync.dma_start(l2[:], offs2)
+        nc.sync.dma_start(xo_w[:].bitcast(I32), as_words(xo_words))
+        nc.sync.dma_start(w_raw["w2"][:].bitcast(I32), as_words(w2_words))
+        nc.sync.dma_start(l1[:], offs)
+        nc.sync.dma_start(w_raw["w0"][:].bitcast(I32), as_words(w0_words))
+        nc.sync.dma_start(w_raw["w"][:].bitcast(I32), as_words(w_words))
+        nc.sync.dma_start(xt_w[:].bitcast(I32), xt_words[0].bitcast(I32))
+        for h in range(2):
+            nc.scalar.dma_start(xo_stage[quad_rows(h), :, :], scale_rows_paired(xo_scales, h))
+        for g, scales in enumerate((w2_scales, w0_scales, w_scales)):
+            for h in range(2):
+                nc.scalar.dma_start(w_stage[quad_rows(h), :, g, :], scale_rows_paired(scales, h))
+        for q in range(4):
+            nc.sync.dma_start(xt_s[quad_rows(q), :].bitcast(I32), scale_rows(xt_scales, q))
+        nc.sync.dma_start(l5[:], offs5)
+        nc.sync.dma_start(sb_t[:], by_feature(sb))
+        nc.sync.dma_start(l4[:], offs4)
+        nc.sync.dma_start(bg_t[:], by_feature(bg))
+        nc.sync.dma_start(l3[:], offs3)
+        nc.sync.dma_start(sa_t[:], by_feature(sa))
+        nc.sync.dma_start(vs_w[:].bitcast(I32), as_words(vs_words))
+        nc.sync.dma_start(l6[:], offs6)
+        for q in range(4):
+            nc.sync.dma_start(vs_s[quad_rows(q), :].bitcast(I32), scale_rows(vs_scales, q))
+        nc.sync.dma_start(l7[:], offs7)
+
+        w_dealt = {g: sbuf(g + "_dealt", [P, PACK, P], U32) for g in w_raw}
+        s_dealt = {g: sbuf(g + "_sdealt", [P, PACK, P], U8) for g in w_raw}
+
+        def deal_words(g):
+            nc.scalar.copy(
+                w_dealt[g][:].rearrange("p t (c i) -> p c t i", i=4),
+                w_raw[g][:].rearrange("p (c i t) -> p c t i", i=4, t=PACK),
+            )
+
+        def deal_scales(g, rows):
+            nc.vector.tensor_copy(s_dealt[g][:], rows.bitcast(U8).rearrange("p (m t) -> p t m", t=PACK))
+
+        xo_gw, xo_gs = sbuf("xo_gw", [P, J], U32), sbuf("xo_gs", [P, J], U8)
+        vs_gw, vs_gs = sbuf("vs_gw", [P, N], U32), sbuf("vs_gs", [P, N], U8)
+
+        nc.vector.tensor_copy(xo_s[: P // 2, :].bitcast(I32), xo_stage[:, 0, :])
+        nc.vector.tensor_copy(xo_s[P // 2 :, :].bitcast(I32), xo_stage[:, 1, :])
+        nc.vector.tensor_copy(xo_gs[:], xo_s[:].indirect(l2[:]))
+        nc.vector.tensor_copy(xo_gw[:], xo_w[:].indirect(l2[:]))
+        nc.vector.tensor_copy(w_stage[P // 2 :, 0], w_stage[: P // 2, 1])
+        for place, g in enumerate(w_raw):
+            deal_words(g)
+            deal_scales(g, w_stage[:, 0, place, :])
+        xt_gw, xt_gs = sbuf("xt_gw", [P, J], U16, tag="w_stage"), sbuf("xt_gs", [P, J], U8)
+        nc.vector.tensor_copy(xt_gw[:], xt_w[:].indirect(l1[:]))
+        nc.vector.tensor_copy(xt_gs[:], xt_s[:].indirect(l1[:]))
+
+        def product(acc, g, fmt, t, words, scales, start, stop):
+            nc.tensor.matmul_mx(
+                out=acc, lhsT=w_dealt[g][:, t, :].bitcast(fmt), lhsT_scale=s_dealt[g][:, t, :],
+                rhs=words, rhs_scale=scales, start=start, stop=stop,
+            )
+
+        b_acc = [psum.tile([P, J], F32, name="b_acc%d" % t, tag="bank%d" % t) for t in range(PACK)]
+        a_acc = [psum.tile([P, J], F32, name="a_acc%d" % t, tag="bank%d" % (PACK + t)) for t in range(PACK)]
+        a_rows = [sbuf("a_rows%d" % t, [P, J], F32) for t in range(PACK)]
+        b_rows = [sbuf("b_rows%d" % t, [P, J], F32) for t in range(PACK)]
+        first = sbuf("first", [P, PACK, O], F32)
+        gate = sbuf("gate", [P, PACK, O], F32)
+        second = sbuf("second", [P, PACK, O], F32)
+        gated = sbuf("gated", [P, PACK, O], F32)
+        hid = sbuf("hid", [P, O, PACK], BF16)
+
+        notes = xo_gw[:].bitcast(E5M2)
+        for t in range(PACK):
+            product(b_acc[t][:], "w2", E4M3, t, notes, xo_gs[:], True, True)
+        for t in range(PACK):
+            product(a_acc[t][:], "w0", E4M3, t, notes, xo_gs[:], True, False)
+        for t in range(PACK):
+            product(a_acc[t][:], "w", E5M2, t, xt_gw[:].bitcast(E2M1), xt_gs[:], False, True)
+
+        for t in range(PACK):
+            nc.scalar.copy(b_rows[t][:], b_acc[t][:])
+        for t in range(PACK):
+            nc.scalar.activation(second[:, t, :], b_rows[t][:].indirect(l5[:]), ACT.Copy, scale=sb_t[:, t : t + 1])
+        for t in range(PACK):
+            nc.vector.tensor_copy(a_rows[t][:], a_acc[t][:])
+        nc.vector.tensor_copy(vs_gw[:], vs_w[:].indirect(l6[:]))
+        nc.vector.tensor_copy(vs_gs[:], vs_s[:].indirect(l6[:]))
+        for t in range(PACK):
+            nc.scalar.activation(
+                gate[:, t, :], a_rows[t][:].indirect(l4[:]), ACT.Sigmoid,
+                bias=bg_t[:, t : t + 1], scale=b_rows[t][:, 0:1],
+            )
+            nc.scalar.activation(first[:, t, :], a_rows[t][:].indirect(l3[:]), ACT.Copy, scale=sa_t[:, t : t + 1])
+            nc.vector.tensor_tensor(gated[:, t, :], first[:, t, :], gate[:, t, :], ALU.mult)
+            if t % 2:
+                pair = slice(t - 1, t + 1)
+                nc.vector.tensor_tensor(
+                    hid[:, :, pair],
+                    gated[:, pair, :].rearrange("p t o -> p o t"),
+                    second[:, pair, :].rearrange("p t o -> p o t"),
+                    ALU.max,
+                )
+
+        hid_w, hid_s = sbuf("hid_w", [P, O], U32), sbuf("hid_s", [P, O], U8)
+        nc.vector.quantize_mx(out=hid_w[:].bitcast(E5M2), scales=hid_s[:], in_=hid[:].rearrange("p o t -> p (o t)"))
+
+        p_acc = [psum.tile([P, O], F32, name="p_acc%d" % h, tag="bank%d" % h) for h in range(2)]
+        p_rows = [sbuf("p_rows%d" % h, [P, O], F32) for h in range(2)]
+        for h in range(2):
+            cols = slice(P * h, P * (h + 1))
+            nc.tensor.matmul_mx(
+                out=p_acc[h][:], lhsT=vs_gw[:, cols].bitcast(E4M3), lhsT_scale=vs_gs[:, cols],
+                rhs=hid_w[:].bitcast(E5M2), rhs_scale=hid_s[:], start=True, stop=True,
+            )
+        nc.vector.tensor_copy(p_rows[0][:], p_acc[0][:])
+        nc.vector.tensor_copy(pages[0][:].indirect(l7[:]), p_rows[0][:])
+        nc.sync.dma_start(out[:P, :], pages[0][:])
+        nc.scalar.copy(p_rows[1][:], p_acc[1][:])
+        nc.scalar.activation(pages[1][:].indirect(l7[:]), p_rows[1][:], ACT.Copy)
+        nc.scalar.dma_start(out[P:, :], pages[1][:])

@@ -89,6 +89,9 @@ def tile_list_slopelead_noted_store_scattered_kernel(
         for g, scales in enumerate((w2_scales, w0_scales, w_scales)):
             for h in range(2):
                 nc.scalar.dma_start(w_stage[quad_rows(h), :, g, :], scale_rows_paired(scales, h))
+        warm_in, warm_out = sbuf("warm_in", [P, 1], F32), sbuf("warm_out", [P, 1], F32)
+        nc.gpsimd.memset(warm_in[:], 0.0)
+        nc.scalar.activation(warm_out[:], warm_in[:], ACT.Sigmoid)
         for q in range(4):
             nc.sync.dma_start(xt_s[quad_rows(q), :].bitcast(I32), scale_rows(xt_scales, q))
         nc.sync.dma_start(l5[:], offs5)

@@ -33,10 +33,14 @@ def tile_list_slopelead_noted_store_scattered_kernel(
     nc = tc.nc
     with ExitStack() as ctx:
         pool = ctx.enter_context(tc.tile_pool(name="held", bufs=1))
+        shared = ctx.enter_context(tc.tile_pool(name="shared", bufs=1))
         psum = ctx.enter_context(tc.psum_pool(name="psum", bufs=1))
 
         def sbuf(name, shape, dtype, tag=""):
             return pool.tile(shape, dtype, name=name, tag=tag, align_bytes=64)
+
+        def placed(name, shape, dtype, offset):
+            return shared.tile(shape, dtype, name=name, offset=offset, align_bytes=64)
 
         def list_tile(name, src):
             return sbuf(name, list(src.shape), U16)
@@ -47,53 +51,50 @@ def tile_list_slopelead_noted_store_scattered_kernel(
         def scale_rows(scales, q):
             return scales[0].bitcast(I32)[PACK * q : PACK * (q + 1), :]
 
-        def scale_rows_paired(scales, h):
-            return scales[0].bitcast(I32).rearrange("(half h i) c -> h i half c", half=2, h=2)[h]
+        def scale_rows_stacked(scales):
+            return scales[0].bitcast(I32).rearrange("(q i) c -> i q c", i=PACK)
 
         def quad_rows(q):
             return slice(QUAD * q, QUAD * q + PACK)
 
         l1, l2, l3, l4 = list_tile("l1", offs), list_tile("l2", offs2), list_tile("l3", offs3), list_tile("l4", offs4)
         l5, l6, l7 = list_tile("l5", offs5), list_tile("l6", offs6), list_tile("l7", offs7)
-        xt_w = sbuf("xt_w", [P, TABLE], U16)
+        xt_w = placed("xt_w", [P, TABLE], U16, 2048)
         xo_w = sbuf("xo_w", [P, TABLE], U32)
         vs_w = sbuf("vs_w", [P, TABLE], U32)
         xt_s = sbuf("xt_s", [P, TABLE], U8)
         xo_s = sbuf("xo_s", [P, TABLE], U8)
-        vs_s = sbuf("vs_s", [P, TABLE], U8)
-        xo_stage = sbuf("xo_stage", [P // 2, 2, TABLE // 4], I32)
-        w_raw = {g: sbuf(g + "_raw", [P, R], U32) for g in ("w2", "w0", "w")}
-        w_stage = sbuf("w_stage", [P, 2, 3, R // 4], I32, tag="w_stage")
+        vs_s = sbuf("vs_s", [P, TABLE], U8, tag="vs_s")
+        xo_stage = sbuf("xo_stage", [PACK, 4, TABLE // 4], I32)
+        w_raw = {g: sbuf(g + "_raw", [P, R], U32) for g in ("w2", "w0")}
+        w_raw["w"] = placed("w_raw", [P, R], U32, 0)
+        w_stage = sbuf("w_stage", [PACK, 4, 3, R // 4], I32)
+        w_planes = placed("w_planes", [P, 3, R // 4], I32, 8192 - 768)
         sa_t, sb_t, bg_t = sbuf("sa_t", [P, PACK], F32), sbuf("sb_t", [P, PACK], F32), sbuf("bg_t", [P, PACK], F32)
-        pages = [sbuf("page%d" % h, [P, E], F32) for h in range(2)]
 
-        nc.vector.memset(xo_stage[:], 0)
-        nc.vector.memset(w_stage[: P // 2], 0)
         nc.vector.memset(xt_s[:].bitcast(I32), 0)
+        nc.vector.memset(xo_s[:].bitcast(I32), 0)
+        nc.vector.memset(w_planes[:], 0)
         nc.vector.memset(vs_s[:].bitcast(I32), 0)
-        for page in pages:
-            nc.vector.memset(page[:], 0.0)
 
         def by_feature(v):
             return v.rearrange("(p t) o -> p (t o)", t=PACK)
 
         nc.sync.dma_start(l2[:], offs2)
-        nc.sync.dma_start(xo_w[:].bitcast(I32), as_words(xo_words))
-        nc.sync.dma_start(w_raw["w2"][:].bitcast(I32), as_words(w2_words))
         nc.sync.dma_start(l1[:], offs)
-        nc.sync.dma_start(w_raw["w0"][:].bitcast(I32), as_words(w0_words))
-        nc.sync.dma_start(w_raw["w"][:].bitcast(I32), as_words(w_words))
-        nc.sync.dma_start(xt_w[:].bitcast(I32), xt_words[0].bitcast(I32))
-        for h in range(2):
-            nc.scalar.dma_start(xo_stage[quad_rows(h), :, :], scale_rows_paired(xo_scales, h))
-        for g, scales in enumerate((w2_scales, w0_scales, w_scales)):
-            for h in range(2):
-                nc.scalar.dma_start(w_stage[quad_rows(h), :, g, :], scale_rows_paired(scales, h))
+        nc.sync.dma_start(xo_stage[:], scale_rows_stacked(xo_scales))
+        nc.sync.dma_start(xo_w[:].bitcast(I32), as_words(xo_words))
+        for place, scales in enumerate((w2_scales, w0_scales, w_scales)):
+            nc.scalar.dma_start(w_stage[:, :, place, :], scale_rows_stacked(scales))
+        nc.scalar.dma_start(w_raw["w2"][:].bitcast(I32), as_words(w2_words))
         warm_in, warm_out = sbuf("warm_in", [P, 1], F32), sbuf("warm_out", [P, 1], F32)
         nc.gpsimd.memset(warm_in[:], 0.0)
         nc.scalar.activation(warm_out[:], warm_in[:], ACT.Sigmoid)
+        nc.sync.dma_start(w_raw["w0"][:].bitcast(I32), as_words(w0_words))
+        nc.sync.dma_start(w_raw["w"][:].bitcast(I32), as_words(w_words))
         for q in range(4):
             nc.sync.dma_start(xt_s[quad_rows(q), :].bitcast(I32), scale_rows(xt_scales, q))
+        nc.sync.dma_start(xt_w[:].bitcast(I32), xt_words[0].bitcast(I32))
         nc.sync.dma_start(l5[:], offs5)
         nc.sync.dma_start(sb_t[:], by_feature(sb))
         nc.sync.dma_start(l4[:], offs4)
@@ -121,17 +122,22 @@ def tile_list_slopelead_noted_store_scattered_kernel(
         xo_gw, xo_gs = sbuf("xo_gw", [P, J], U32), sbuf("xo_gs", [P, J], U8)
         vs_gw, vs_gs = sbuf("vs_gw", [P, N], U32), sbuf("vs_gs", [P, N], U8)
 
-        nc.vector.tensor_copy(xo_s[: P // 2, :].bitcast(I32), xo_stage[:, 0, :])
-        nc.vector.tensor_copy(xo_s[P // 2 :, :].bitcast(I32), xo_stage[:, 1, :])
+        xt_gw, xt_gs = sbuf("xt_gw", [P, J], U16), sbuf("xt_gs", [P, J], U8)
+        for q in range(4):
+            nc.vector.tensor_copy(xo_s[quad_rows(q), :].bitcast(I32), xo_stage[:, q, :])
+            nc.vector.tensor_copy(w_planes[quad_rows(q)], w_stage[:, q])
+        for g in w_raw:
+            deal_words(g)
+        deal_scales("w2", w_planes[:, 0, :])
         nc.vector.tensor_copy(xo_gs[:], xo_s[:].indirect(l2[:]))
         nc.vector.tensor_copy(xo_gw[:], xo_w[:].indirect(l2[:]))
-        nc.vector.tensor_copy(w_stage[P // 2 :, 0], w_stage[: P // 2, 1])
-        for place, g in enumerate(w_raw):
-            deal_words(g)
-            deal_scales(g, w_stage[:, 0, place, :])
-        xt_gw, xt_gs = sbuf("xt_gw", [P, J], U16, tag="w_stage"), sbuf("xt_gs", [P, J], U8)
-        nc.vector.tensor_copy(xt_gw[:], xt_w[:].indirect(l1[:]))
+        deal_scales("w0", w_planes[:, 1, :])
+        deal_scales("w", w_planes[:, 2, :])
+        pages = [placed("page%d" % h, [P, E], F32, 4096 * (h + 1)) for h in range(2)]
+        for page in pages:
+            nc.gpsimd.memset(page[:], 0.0)
         nc.vector.tensor_copy(xt_gs[:], xt_s[:].indirect(l1[:]))
+        nc.vector.tensor_copy(xt_gw[:], xt_w[:].indirect(l1[:]))
 
         def product(acc, g, fmt, t, words, scales, start, stop):
             nc.tensor.matmul_mx(
@@ -140,31 +146,32 @@ def tile_list_slopelead_noted_store_scattered_kernel(
             )
 
         b_acc = [psum.tile([P, J], F32, name="b_acc%d" % t, tag="bank%d" % t) for t in range(PACK)]
-        a_acc = [psum.tile([P, J], F32, name="a_acc%d" % t, tag="bank%d" % (PACK + t)) for t in range(PACK)]
         a_rows = [sbuf("a_rows%d" % t, [P, J], F32) for t in range(PACK)]
-        b_rows = [sbuf("b_rows%d" % t, [P, J], F32) for t in range(PACK)]
+        b_rows = [placed("b_rows%d" % t, [P, J], F32, 1024 * t) for t in range(PACK)]
         first = sbuf("first", [P, PACK, O], F32)
         gate = sbuf("gate", [P, PACK, O], F32)
         second = sbuf("second", [P, PACK, O], F32)
-        gated = sbuf("gated", [P, PACK, O], F32)
         hid = sbuf("hid", [P, O, PACK], BF16)
 
         notes = xo_gw[:].bitcast(E5M2)
         for t in range(PACK):
             product(b_acc[t][:], "w2", E4M3, t, notes, xo_gs[:], True, True)
         for t in range(PACK):
+            if t < 2:
+                nc.scalar.copy(b_rows[t][:], b_acc[t][:])
+            else:
+                nc.vector.tensor_copy(b_rows[t][:], b_acc[t][:])
+        a_acc = [psum.tile([P, J], F32, name="a_acc%d" % t, tag="bank%d" % (4, 5, 2, 3)[t]) for t in range(PACK)]
+        for t in range(PACK):
             product(a_acc[t][:], "w0", E4M3, t, notes, xo_gs[:], True, False)
-        for t in range(PACK):
             product(a_acc[t][:], "w", E5M2, t, xt_gw[:].bitcast(E2M1), xt_gs[:], False, True)
-
-        for t in range(PACK):
-            nc.scalar.copy(b_rows[t][:], b_acc[t][:])
         for t in range(PACK):
             nc.scalar.activation(second[:, t, :], b_rows[t][:].indirect(l5[:]), ACT.Copy, scale=sb_t[:, t : t + 1])
         for t in range(PACK):
             nc.vector.tensor_copy(a_rows[t][:], a_acc[t][:])
         nc.vector.tensor_copy(vs_gw[:], vs_w[:].indirect(l6[:]))
         nc.vector.tensor_copy(vs_gs[:], vs_s[:].indirect(l6[:]))
+        gated = sbuf("gated", [P, PACK, O], F32, tag="vs_s")
         for t in range(PACK):
             nc.scalar.activation(
                 gate[:, t, :], a_rows[t][:].indirect(l4[:]), ACT.Sigmoid,

@@ -54,6 +54,9 @@ def tile_list_slopelead_noted_store_scattered_kernel(
         def scale_rows_stacked(scales):
             return scales[0].bitcast(I32).rearrange("(q i) c -> i q c", i=PACK)
 
+        def scale_rows_paired(scales, h):
+            return scales[0].bitcast(I32).rearrange("(half h i) c -> h i half c", half=2, h=2)[h]
+
         def quad_rows(q):
             return slice(QUAD * q, QUAD * q + PACK)
 
@@ -65,16 +68,16 @@ def tile_list_slopelead_noted_store_scattered_kernel(
         xt_s = sbuf("xt_s", [P, TABLE], U8)
         xo_s = sbuf("xo_s", [P, TABLE], U8)
         vs_s = sbuf("vs_s", [P, TABLE], U8, tag="vs_s")
-        xo_stage = sbuf("xo_stage", [PACK, 4, TABLE // 4], I32)
+        xo_stage = sbuf("xo_stage", [P, 2, TABLE // 4], I32)
         w_raw = {g: sbuf(g + "_raw", [P, R], U32) for g in ("w2", "w0")}
         w_raw["w"] = placed("w_raw", [P, R], U32, 0)
-        w_stage = sbuf("w_stage", [PACK, 4, 3, R // 4], I32)
-        w_planes = placed("w_planes", [P, 3, R // 4], I32, 8192 - 768)
+        w_stage = sbuf("w_stage", [P, 4, 3, R // 4], I32)
+        w_planes = w_stage[:, 0]
         sa_t, sb_t, bg_t = sbuf("sa_t", [P, PACK], F32), sbuf("sb_t", [P, PACK], F32), sbuf("bg_t", [P, PACK], F32)
 
+        nc.vector.memset(w_planes, 0)
+        nc.vector.memset(xo_stage[P // 2 :], 0)
         nc.vector.memset(xt_s[:].bitcast(I32), 0)
-        nc.vector.memset(xo_s[:].bitcast(I32), 0)
-        nc.vector.memset(w_planes[:], 0)
         nc.vector.memset(vs_s[:].bitcast(I32), 0)
 
         def by_feature(v):
@@ -82,14 +85,18 @@ def tile_list_slopelead_noted_store_scattered_kernel(
 
         nc.sync.dma_start(l2[:], offs2)
         nc.sync.dma_start(l1[:], offs)
-        nc.sync.dma_start(xo_stage[:], scale_rows_stacked(xo_scales))
-        nc.sync.dma_start(xo_w[:].bitcast(I32), as_words(xo_words))
         for place, scales in enumerate((w2_scales, w0_scales, w_scales)):
-            nc.scalar.dma_start(w_stage[:, :, place, :], scale_rows_stacked(scales))
-        nc.scalar.dma_start(w_raw["w2"][:].bitcast(I32), as_words(w2_words))
+            nc.scalar.dma_start(w_stage[:PACK, :, place, :], scale_rows_stacked(scales))
+        for h, queue in enumerate((nc.sync, nc.scalar)):
+            queue.dma_start(xo_stage[quad_rows(2 + h)], scale_rows_paired(xo_scales, h))
+        nc.sync.dma_start(xo_w[:].bitcast(I32), as_words(xo_words))
+        nc.sync.dma_start(w_raw["w2"][:].bitcast(I32), as_words(w2_words))
         warm_in, warm_out = sbuf("warm_in", [P, 1], F32), sbuf("warm_out", [P, 1], F32)
-        nc.gpsimd.memset(warm_in[:], 0.0)
+        nc.vector.memset(warm_in[:], 0.0)
         nc.scalar.activation(warm_out[:], warm_in[:], ACT.Sigmoid)
+        pages = [sbuf("page%d" % h, [P, E], F32) for h in range(2)]
+        for page in pages:
+            nc.vector.memset(page[:], 0.0)
         nc.sync.dma_start(w_raw["w0"][:].bitcast(I32), as_words(w0_words))
         nc.sync.dma_start(w_raw["w"][:].bitcast(I32), as_words(w_words))
         for q in range(4):
@@ -123,9 +130,10 @@ def tile_list_slopelead_noted_store_scattered_kernel(
         vs_gw, vs_gs = sbuf("vs_gw", [P, N], U32), sbuf("vs_gs", [P, N], U8)
 
         xt_gw, xt_gs = sbuf("xt_gw", [P, J], U16), sbuf("xt_gs", [P, J], U8)
-        for q in range(4):
-            nc.vector.tensor_copy(xo_s[quad_rows(q), :].bitcast(I32), xo_stage[:, q, :])
-            nc.vector.tensor_copy(w_planes[quad_rows(q)], w_stage[:, q])
+        nc.vector.tensor_copy(xo_s[P // 2 :, :].bitcast(I32), xo_stage[P // 2 :, 1, :])
+        nc.vector.tensor_copy(xo_s[: P // 2, :].bitcast(I32), xo_stage[P // 2 :, 0, :])
+        for q in range(1, 4):
+            nc.vector.tensor_copy(w_stage[quad_rows(q), 0], w_stage[:PACK, q])
         for g in w_raw:
             deal_words(g)
         deal_scales("w2", w_planes[:, 0, :])
@@ -133,9 +141,6 @@ def tile_list_slopelead_noted_store_scattered_kernel(
         nc.vector.tensor_copy(xo_gw[:], xo_w[:].indirect(l2[:]))
         deal_scales("w0", w_planes[:, 1, :])
         deal_scales("w", w_planes[:, 2, :])
-        pages = [placed("page%d" % h, [P, E], F32, 4096 * (h + 1)) for h in range(2)]
-        for page in pages:
-            nc.gpsimd.memset(page[:], 0.0)
         nc.vector.tensor_copy(xt_gs[:], xt_s[:].indirect(l1[:]))
         nc.vector.tensor_copy(xt_gw[:], xt_w[:].indirect(l1[:]))
 

from contextlib import ExitStack

import concourse.mybir as mybir

F32 = mybir.dt.float32
BF16 = mybir.dt.bfloat16
I32 = mybir.dt.int32
U32 = mybir.dt.uint32
U16 = mybir.dt.uint16
U8 = mybir.dt.uint8
E4M3 = mybir.dt.float8_e4m3fn_x4
E5M2 = mybir.dt.float8_e5m2_x4
E2M1 = mybir.dt.float4_e2m1fn_x4
ACT = mybir.ActivationFunctionType
ALU = mybir.AluOpType

P = 128
PACK = 4
QUAD = 32
TABLE = 1024
R = 512
J = 256
O = 128
N = 256
E = 1024
FLOPS = 2 * (3 * 512 * R * J + R * N * O)


def tile_list_slopelead_noted_store_scattered_kernel(
    tc, xt_words, xt_scales, xo_words, xo_scales, w_words, w_scales, w0_words, w0_scales, w2_words, w2_scales,
    sa, sb, bg, vs_words, vs_scales, offs, offs2, offs3, offs4, offs5, offs6, offs7, out,
):
    nc = tc.nc
    with ExitStack() as ctx:
        pool = ctx.enter_context(tc.tile_pool(name="held", bufs=1))
        shared = ctx.enter_context(tc.tile_pool(name="shared", bufs=1))
        psum = ctx.enter_context(tc.psum_pool(name="psum", bufs=1))

        def sbuf(name, shape, dtype, tag=""):
            return pool.tile(shape, dtype, name=name, tag=tag, align_bytes=64)

        def placed(name, shape, dtype, offset):
            return shared.tile(shape, dtype, name=name, offset=offset, align_bytes=64)

        def list_tile(name, src):
            return sbuf(name, list(src.shape), U16)

        def as_words(words):
            return words[0].rearrange("p c r -> p (c r)").bitcast(I32)

        def scale_rows(scales, q):
            return scales[0].bitcast(I32)[PACK * q : PACK * (q + 1), :]

        def scale_rows_stacked(scales):
            return scales[0].bitcast(I32).rearrange("(q i) c -> i q c", i=PACK)

        def scale_rows_paired(scales, h):
            return scales[0].bitcast(I32).rearrange("(half h i) c -> h i half c", half=2, h=2)[h]

        def quad_rows(q):
            return slice(QUAD * q, QUAD * q + PACK)

        l1, l2, l3, l4 = list_tile("l1", offs), list_tile("l2", offs2), list_tile("l3", offs3), list_tile("l4", offs4)
        l5, l6, l7 = list_tile("l5", offs5), list_tile("l6", offs6), list_tile("l7", offs7)
        xt_w = placed("xt_w", [P, TABLE], U16, 2048)
        xo_w = sbuf("xo_w", [P, TABLE], U32)
        vs_w = sbuf("vs_w", [P, TABLE], U32)
        xt_s = sbuf("xt_s", [P, TABLE], U8)
        xo_s = sbuf("xo_s", [P, TABLE], U8)
        vs_s = sbuf("vs_s", [P, TABLE], U8, tag="vs_s")
        xo_stage = sbuf("xo_stage", [P, 2, TABLE // 4], I32)
        w_raw = {g: sbuf(g + "_raw", [P, R], U32) for g in ("w2", "w0")}
        w_raw["w"] = placed("w_raw", [P, R], U32, 0)
        w_stage = sbuf("w_stage", [P, 4, 3, R // 4], I32)
        w_planes = w_stage[:, 0]
        sa_t, sb_t, bg_t = sbuf("sa_t", [P, PACK], F32), sbuf("sb_t", [P, PACK], F32), sbuf("bg_t", [P, PACK], F32)

        nc.vector.memset(w_planes, 0)
        nc.vector.memset(xo_stage[P // 2 :], 0)
        nc.vector.memset(xt_s[:].bitcast(I32), 0)
        nc.vector.memset(vs_s[:].bitcast(I32), 0)

        def by_feature(v):
            return v.rearrange("(p t) o -> p (t o)", t=PACK)

        nc.sync.dma_start(l2[:], offs2)
        nc.sync.dma_start(l1[:], offs)
        for place, scales in enumerate((w2_scales, w0_scales, w_scales)):
            nc.scalar.dma_start(w_stage[:PACK, :, place, :], scale_rows_stacked(scales))
        for h, queue in enumerate((nc.sync, nc.scalar)):
            queue.dma_start(xo_stage[quad_rows(2 + h)], scale_rows_paired(xo_scales, h))
        nc.sync.dma_start(xo_w[:].bitcast(I32), as_words(xo_words))
        nc.sync.dma_start(w_raw["w2"][:].bitcast(I32), as_words(w2_words))
        warm_in, warm_out = sbuf("warm_in", [P, 1], F32), sbuf("warm_out", [P, 1], F32)
        nc.vector.memset(warm_in[:], 0.0)
        nc.scalar.activation(warm_out[:], warm_in[:], ACT.Sigmoid)
        pages = [sbuf("page%d" % h, [P, E], F32) for h in range(2)]
        for page in pages:
            nc.vector.memset(page[:], 0.0)
        nc.sync.dma_start(w_raw["w0"][:].bitcast(I32), as_words(w0_words))
        nc.sync.dma_start(w_raw["w"][:].bitcast(I32), as_words(w_words))
        for q in range(4):
            nc.sync.dma_start(xt_s[quad_rows(q), :].bitcast(I32), scale_rows(xt_scales, q))
        nc.sync.dma_start(xt_w[:].bitcast(I32), xt_words[0].bitcast(I32))
        nc.sync.dma_start(l5[:], offs5)
        nc.sync.dma_start(sb_t[:], by_feature(sb))
        nc.sync.dma_start(l4[:], offs4)
        nc.sync.dma_start(bg_t[:], by_feature(bg))
        nc.sync.dma_start(l3[:], offs3)
        nc.sync.dma_start(sa_t[:], by_feature(sa))
        nc.sync.dma_start(vs_w[:].bitcast(I32), as_words(vs_words))
        nc.sync.dma_start(l6[:], offs6)
        for q in range(4):
            nc.sync.dma_start(vs_s[quad_rows(q), :].bitcast(I32), scale_rows(vs_scales, q))
        nc.sync.dma_start(l7[:], offs7)

        w_dealt = {g: sbuf(g + "_dealt", [P, PACK, P], U32) for g in w_raw}
        s_dealt = {g: sbuf(g + "_sdealt", [P, PACK, P], U8) for g in w_raw}

        def deal_words(g):
            nc.scalar.copy(
                w_dealt[g][:].rearrange("p t (c i) -> p c t i", i=4),
                w_raw[g][:].rearrange("p (c i t) -> p c t i", i=4, t=PACK),
            )

        def deal_scales(g, rows):
            nc.vector.tensor_copy(s_dealt[g][:], rows.bitcast(U8).rearrange("p (m t) -> p t m", t=PACK))

        xo_gw, xo_gs = sbuf("xo_gw", [P, J], U32), sbuf("xo_gs", [P, J], U8)
        vs_gw, vs_gs = sbuf("vs_gw", [P, N], U32), sbuf("vs_gs", [P, N], U8)

        xt_gw, xt_gs = sbuf("xt_gw", [P, J], U16), sbuf("xt_gs", [P, J], U8)
        nc.vector.tensor_copy(xo_s[P // 2 :, :].bitcast(I32), xo_stage[P // 2 :, 1, :])
        nc.vector.tensor_copy(xo_s[: P // 2, :].bitcast(I32), xo_stage[P // 2 :, 0, :])
        for q in range(1, 4):
            nc.vector.tensor_copy(w_stage[quad_rows(q), 0], w_stage[:PACK, q])
        for g in w_raw:
            deal_words(g)
        deal_scales("w2", w_planes[:, 0, :])
        nc.vector.tensor_copy(xo_gs[:], xo_s[:].indirect(l2[:]))
        nc.vector.tensor_copy(xo_gw[:], xo_w[:].indirect(l2[:]))
        deal_scales("w0", w_planes[:, 1, :])
        deal_scales("w", w_planes[:, 2, :])
        nc.vector.tensor_copy(xt_gs[:], xt_s[:].indirect(l1[:]))
        nc.vector.tensor_copy(xt_gw[:], xt_w[:].indirect(l1[:]))

        def product(acc, g, fmt, t, words, scales, start, stop):
            nc.tensor.matmul_mx(
                out=acc, lhsT=w_dealt[g][:, t, :].bitcast(fmt), lhsT_scale=s_dealt[g][:, t, :],
                rhs=words, rhs_scale=scales, start=start, stop=stop,
            )

        b_acc = [psum.tile([P, J], F32, name="b_acc%d" % t, tag="bank%d" % t) for t in range(PACK)]
        a_rows = [sbuf("a_rows%d" % t, [P, J], F32) for t in range(PACK)]
        b_rows = [placed("b_rows%d" % t, [P, J], F32, 1024 * t) for t in range(PACK)]
        first = sbuf("first", [P, PACK, O], F32)
        gate = sbuf("gate", [P, PACK, O], F32)
        second = sbuf("second", [P, PACK, O], F32)
        hid = sbuf("hid", [P, O, PACK], BF16)

        notes = xo_gw[:].bitcast(E5M2)
        for t in range(PACK):
            product(b_acc[t][:], "w2", E4M3, t, notes, xo_gs[:], True, True)
        for t in range(PACK):
            if t < 2:
                nc.scalar.copy(b_rows[t][:], b_acc[t][:])
            else:
                nc.vector.tensor_copy(b_rows[t][:], b_acc[t][:])
        a_acc = [psum.tile([P, J], F32, name="a_acc%d" % t, tag="bank%d" % (4, 5, 2, 3)[t]) for t in range(PACK)]
        for t in range(PACK):
            product(a_acc[t][:], "w0", E4M3, t, notes, xo_gs[:], True, False)
            product(a_acc[t][:], "w", E5M2, t, xt_gw[:].bitcast(E2M1), xt_gs[:], False, True)
        for t in range(PACK):
            nc.scalar.activation(second[:, t, :], b_rows[t][:].indirect(l5[:]), ACT.Copy, scale=sb_t[:, t : t + 1])
        for t in range(PACK):
            nc.vector.tensor_copy(a_rows[t][:], a_acc[t][:])
        nc.vector.tensor_copy(vs_gw[:], vs_w[:].indirect(l6[:]))
        nc.vector.tensor_copy(vs_gs[:], vs_s[:].indirect(l6[:]))
        gated = sbuf("gated", [P, PACK, O], F32, tag="vs_s")
        for t in range(PACK):
            nc.scalar.activation(
                gate[:, t, :], a_rows[t][:].indirect(l4[:]), ACT.Sigmoid,
                bias=bg_t[:, t : t + 1], scale=b_rows[t][:, 0:1],
            )
            nc.scalar.activation(first[:, t, :], a_rows[t][:].indirect(l3[:]), ACT.Copy, scale=sa_t[:, t : t + 1])
            nc.vector.tensor_tensor(gated[:, t, :], first[:, t, :], gate[:, t, :], ALU.mult)
            if t % 2:
                pair = slice(t - 1, t + 1)
                nc.vector.tensor_tensor(
                    hid[:, :, pair],
                    gated[:, pair, :].rearrange("p t o -> p o t"),
                    second[:, pair, :].rearrange("p t o -> p o t"),
                    ALU.max,
                )

        hid_w, hid_s = sbuf("hid_w", [P, O], U32), sbuf("hid_s", [P, O], U8)
        nc.vector.quantize_mx(out=hid_w[:].bitcast(E5M2), scales=hid_s[:], in_=hid[:].rearrange("p o t -> p (o t)"))

        p_acc = [psum.tile([P, O], F32, name="p_acc%d" % h, tag="bank%d" % h) for h in range(2)]
        p_rows = [sbuf("p_rows%d" % h, [P, O], F32) for h in range(2)]
        for h in range(2):
            cols = slice(P * h, P * (h + 1))
            nc.tensor.matmul_mx(
                out=p_acc[h][:], lhsT=vs_gw[:, cols].bitcast(E4M3), lhsT_scale=vs_gs[:, cols],
                rhs=hid_w[:].bitcast(E5M2), rhs_scale=hid_s[:], start=True, stop=True,
            )
        nc.vector.tensor_copy(p_rows[0][:], p_acc[0][:])
        nc.vector.tensor_copy(pages[0][:].indirect(l7[:]), p_rows[0][:])
        nc.sync.dma_start(out[:P, :], pages[0][:])
        nc.scalar.copy(p_rows[1][:], p_acc[1][:])
        nc.scalar.activation(pages[1][:].indirect(l7[:]), p_rows[1][:], ACT.Copy)
        nc.scalar.dma_start(out[P:, :], pages[1][:])
